import numpy as np
import ml_dtypes

BF16 = ml_dtypes.bfloat16


def bf(x):
    return np.asarray(x, np.float32).astype(BF16)


def f32(x):
    return np.asarray(x, np.float32)


def f64(x):
    return np.asarray(x).astype(np.float64)


def striped(idx):
    return np.tile(idx.reshape(-1, 16).T, (8, 1))


S, K, M, N = 1024, 512, 128, 1024


def setup_inputs():
    return {"table": bf(np.random.standard_normal((K, S))), "w": bf(np.random.standard_normal((K, M)) / np.sqrt(K)), "offs": striped(np.random.permutation(S))}


def reference(table, w, offs):
    idx = offs[:16].T.reshape(-1)
    x = f64(table)[:, idx]
    y = f64(w).T @ x
    return y

@@ -1,0 +1,49 @@
+import concourse.mybir as mybir
+
+BF16, F32, U16 = mybir.dt.bfloat16, mybir.dt.float32, mybir.dt.uint16
+
+P = 128
+S = 1024
+K = 512
+M = 128
+N = 1024
+K_BLOCKS = K // P
+PIECE = 512
+PIECE_COLS = PIECE // 16
+
+FLOPS = 2 * K * M * N
+
+
+def tile_gather_matmul_kernel(tc, table, w, offs, out):
+    nc = tc.nc
+    with (
+        tc.tile_pool(name="held", bufs=1) as held,
+        tc.psum_pool(name="psum", bufs=1) as psum,
+    ):
+        offsets = held.tile([P, N // 16], U16, name="offsets")
+        nc.sync.dma_start(offsets[:], offs)
+
+        weights = held.tile([P, K_BLOCKS, M], BF16, name="weights")
+        nc.scalar.dma_start(weights[:], w.rearrange("(b p) m -> p b m", p=P))
+
+        blocks = []
+        for b in range(K_BLOCKS):
+            block = held.tile([P, S], BF16, name=f"block{b}")
+            queue = nc.sync if b % 2 == 0 else nc.scalar
+            queue.dma_start(block[:], table[b * P : (b + 1) * P, :])
+            blocks.append(block)
+
+        for piece in range(N // PIECE):
+            piece_offsets = offsets[:, piece * PIECE_COLS : (piece + 1) * PIECE_COLS]
+            bank = psum.tile([P, PIECE], F32, name=f"bank{piece}")
+            for b in range(K_BLOCKS):
+                nc.tensor.matmul(
+                    bank[:],
+                    weights[:, b, :],
+                    blocks[b][:].indirect(piece_offsets),
+                    start=(b == 0),
+                    stop=(b == K_BLOCKS - 1),
+                )
+            staged = held.tile([P, PIECE], F32, name=f"staged{piece}")
+            nc.vector.tensor_copy(staged[:], bank[:])
+            nc.sync.dma_start(out[:, piece * PIECE : (piece + 1) * PIECE], staged[:])

@@ -10,6 +10,7 @@ N = 1024
 K_BLOCKS = K // P
 PIECE = 512
 PIECE_COLS = PIECE // 16
+WARM_UPS = 4
 
 FLOPS = 2 * K * M * N
 
@@ -20,6 +21,12 @@ def tile_gather_matmul_kernel(tc, table, w, offs, out):
         tc.tile_pool(name="held", bufs=1) as held,
         tc.psum_pool(name="psum", bufs=1) as psum,
     ):
+        zeros = held.tile([P, PIECE], BF16, name="zeros")
+        nc.vector.memset(zeros[:], 0.0)
+        warm_bank = psum.tile([P, PIECE], F32, name="warm_bank")
+        for i in range(WARM_UPS):
+            nc.tensor.matmul(warm_bank[:], zeros[:, 0:P], zeros[:], start=True, stop=True)
+
         offsets = held.tile([P, N // 16], U16, name="offsets")
         nc.sync.dma_start(offsets[:], offs)
 

@@ -8,9 +8,9 @@ K = 512
 M = 128
 N = 1024
 K_BLOCKS = K // P
-PIECE = 512
-PIECE_COLS = PIECE // 16
-WARM_UPS = 4
+BANK = 512
+PIECES = (512, 384, 128)
+assert sum(PIECES) == N and max(PIECES) <= BANK
 
 FLOPS = 2 * K * M * N
 
@@ -21,36 +21,34 @@ def tile_gather_matmul_kernel(tc, table, w, offs, out):
         tc.tile_pool(name="held", bufs=1) as held,
         tc.psum_pool(name="psum", bufs=1) as psum,
     ):
-        zeros = held.tile([P, PIECE], BF16, name="zeros")
-        nc.vector.memset(zeros[:], 0.0)
-        warm_bank = psum.tile([P, PIECE], F32, name="warm_bank")
-        for i in range(WARM_UPS):
-            nc.tensor.matmul(warm_bank[:], zeros[:, 0:P], zeros[:], start=True, stop=True)
-
         offsets = held.tile([P, N // 16], U16, name="offsets")
         nc.sync.dma_start(offsets[:], offs)
 
         weights = held.tile([P, K_BLOCKS, M], BF16, name="weights")
-        nc.scalar.dma_start(weights[:], w.rearrange("(b p) m -> p b m", p=P))
+        nc.scalar.dma_start(weights[:], w.rearrange("(p b) m -> p b m", b=K_BLOCKS))
 
+        table_blocks = table.rearrange("(p b) s -> b p s", b=K_BLOCKS)
         blocks = []
         for b in range(K_BLOCKS):
             block = held.tile([P, S], BF16, name=f"block{b}")
-            queue = nc.sync if b % 2 == 0 else nc.scalar
-            queue.dma_start(block[:], table[b * P : (b + 1) * P, :])
+            nc.sync.dma_start(block[:], table_blocks[b])
             blocks.append(block)
 
-        for piece in range(N // PIECE):
-            piece_offsets = offsets[:, piece * PIECE_COLS : (piece + 1) * PIECE_COLS]
-            bank = psum.tile([P, PIECE], F32, name=f"bank{piece}")
-            for b in range(K_BLOCKS):
+        first = 0
+        for i, size in enumerate(PIECES):
+            piece_offsets = offsets[:, first // 16 : (first + size) // 16]
+            bank = psum.tile([P, size], F32, name=f"bank{i}")
+            order = list(range(K_BLOCKS)) if i == 0 else list(reversed(range(K_BLOCKS)))
+            for b in order:
                 nc.tensor.matmul(
                     bank[:],
                     weights[:, b, :],
                     blocks[b][:].indirect(piece_offsets),
-                    start=(b == 0),
-                    stop=(b == K_BLOCKS - 1),
+                    start=(b == order[0]),
+                    stop=(b == order[-1]),
                 )
-            staged = held.tile([P, PIECE], F32, name=f"staged{piece}")
+            staged = held.tile([P, size], F32, name=f"staged{i}")
             nc.vector.tensor_copy(staged[:], bank[:])
-            nc.sync.dma_start(out[:, piece * PIECE : (piece + 1) * PIECE], staged[:])
+            queue = nc.sync if i % 2 == 0 else nc.scalar
+            queue.dma_start(out[:, first : first + size], staged[:])
+            first += size

@@ -9,8 +9,9 @@ M = 128
 N = 1024
 K_BLOCKS = K // P
 BANK = 512
-PIECES = (512, 384, 128)
-assert sum(PIECES) == N and max(PIECES) <= BANK
+PIECES = 4
+PIECE = N // PIECES
+assert PIECE <= BANK
 
 FLOPS = 2 * K * M * N
 
@@ -34,21 +35,24 @@ def tile_gather_matmul_kernel(tc, table, w, offs, out):
             nc.sync.dma_start(block[:], table_blocks[b])
             blocks.append(block)
 
-        first = 0
-        for i, size in enumerate(PIECES):
-            piece_offsets = offsets[:, first // 16 : (first + size) // 16]
-            bank = psum.tile([P, size], F32, name=f"bank{i}")
-            order = list(range(K_BLOCKS)) if i == 0 else list(reversed(range(K_BLOCKS)))
-            for b in order:
+        banks = [psum.tile([P, PIECE], F32, name=f"bank{i}") for i in range(PIECES)]
+
+        for b in range(K_BLOCKS):
+            for i in range(PIECES):
                 nc.tensor.matmul(
-                    bank[:],
+                    banks[i][:],
                     weights[:, b, :],
-                    blocks[b][:].indirect(piece_offsets),
-                    start=(b == order[0]),
-                    stop=(b == order[-1]),
+                    blocks[b][:].indirect(offsets[:, i * PIECE // 16 : (i + 1) * PIECE // 16]),
+                    start=(b == 0),
+                    stop=(b == K_BLOCKS - 1),
                 )
-            staged = held.tile([P, size], F32, name=f"staged{i}")
-            nc.vector.tensor_copy(staged[:], bank[:])
-            queue = nc.sync if i % 2 == 0 else nc.scalar
-            queue.dma_start(out[:, first : first + size], staged[:])
-            first += size
+
+        for i in range(PIECES):
+            staged = held.tile([P, PIECE], F32, name=f"staged{i}")
+            columns = out[:, i * PIECE : (i + 1) * PIECE]
+            if i % 2 == 0:
+                nc.vector.tensor_copy(staged[:], banks[i][:])
+                nc.sync.dma_start(columns, staged[:])
+            else:
+                nc.scalar.copy(staged[:], banks[i][:])
+                nc.scalar.dma_start(columns, staged[:])

@@ -9,9 +9,8 @@ M = 128
 N = 1024
 K_BLOCKS = K // P
 BANK = 512
-PIECES = 4
-PIECE = N // PIECES
-assert PIECE <= BANK
+PIECES = (512, 384, 128)
+assert sum(PIECES) == N and max(PIECES) <= BANK
 
 FLOPS = 2 * K * M * N
 
@@ -26,33 +25,29 @@ def tile_gather_matmul_kernel(tc, table, w, offs, out):
         nc.sync.dma_start(offsets[:], offs)
 
         weights = held.tile([P, K_BLOCKS, M], BF16, name="weights")
-        nc.scalar.dma_start(weights[:], w.rearrange("(p b) m -> p b m", b=K_BLOCKS))
+        nc.scalar.dma_start(weights[:], w.rearrange("(b p) m -> p b m", p=P))
 
-        table_blocks = table.rearrange("(p b) s -> b p s", b=K_BLOCKS)
         blocks = []
         for b in range(K_BLOCKS):
             block = held.tile([P, S], BF16, name=f"block{b}")
-            nc.sync.dma_start(block[:], table_blocks[b])
+            queue = nc.sync if b % 2 == 0 else nc.scalar
+            queue.dma_start(block[:], table[b * P : (b + 1) * P, :])
             blocks.append(block)
 
-        banks = [psum.tile([P, PIECE], F32, name=f"bank{i}") for i in range(PIECES)]
-
-        for b in range(K_BLOCKS):
-            for i in range(PIECES):
+        first = 0
+        for i, size in enumerate(PIECES):
+            piece_offsets = offsets[:, first // 16 : (first + size) // 16]
+            bank = psum.tile([P, size], F32, name=f"bank{i}")
+            for b in range(K_BLOCKS):
                 nc.tensor.matmul(
-                    banks[i][:],
+                    bank[:],
                     weights[:, b, :],
-                    blocks[b][:].indirect(offsets[:, i * PIECE // 16 : (i + 1) * PIECE // 16]),
+                    blocks[b][:].indirect(piece_offsets),
                     start=(b == 0),
                     stop=(b == K_BLOCKS - 1),
                 )
-
-        for i in range(PIECES):
-            staged = held.tile([P, PIECE], F32, name=f"staged{i}")
-            columns = out[:, i * PIECE : (i + 1) * PIECE]
-            if i % 2 == 0:
-                nc.vector.tensor_copy(staged[:], banks[i][:])
-                nc.sync.dma_start(columns, staged[:])
-            else:
-                nc.scalar.copy(staged[:], banks[i][:])
-                nc.scalar.dma_start(columns, staged[:])
+            staged = held.tile([P, size], F32, name=f"staged{i}")
+            nc.vector.tensor_copy(staged[:], bank[:])
+            queue = nc.sync if i % 2 == 0 else nc.scalar
+            queue.dma_start(out[:, first : first + size], staged[:])
+            first += size

@@ -24,27 +24,32 @@ def tile_gather_matmul_kernel(tc, table, w, offs, out):
         offsets = held.tile([P, N // 16], U16, name="offsets")
         nc.sync.dma_start(offsets[:], offs)
 
-        weights = held.tile([P, K_BLOCKS, M], BF16, name="weights")
-        nc.scalar.dma_start(weights[:], w.rearrange("(b p) m -> p b m", p=P))
+        blocks = [held.tile([P, S], BF16, name=f"block{b}") for b in range(K_BLOCKS)]
+        nc.scalar.dma_start(blocks[0][:], table[0:P, :])
 
-        blocks = []
-        for b in range(K_BLOCKS):
-            block = held.tile([P, S], BF16, name=f"block{b}")
-            queue = nc.sync if b % 2 == 0 else nc.scalar
-            queue.dma_start(block[:], table[b * P : (b + 1) * P, :])
-            blocks.append(block)
+        first_weights = held.tile([P, M], BF16, name="first_weights")
+        nc.sync.dma_start(first_weights[:], w[0:P, :])
+        later_weights = held.tile([P, K_BLOCKS - 1, M], BF16, name="later_weights")
+        nc.scalar.dma_start(later_weights[:], w[P:K, :].rearrange("(b p) m -> p b m", p=P))
+        weights = [first_weights[:]] + [later_weights[:, b - 1, :] for b in range(1, K_BLOCKS)]
 
+        for b in range(1, K_BLOCKS):
+            nc.scalar.dma_start(blocks[b][:], table[b * P : (b + 1) * P, :])
+
+        arriving = list(range(K_BLOCKS))
+        as_they_arrive = (K_BLOCKS, 1, 0)
         first = 0
         for i, size in enumerate(PIECES):
             piece_offsets = offsets[:, first // 16 : (first + size) // 16]
             bank = psum.tile([P, size], F32, name=f"bank{i}")
-            for b in range(K_BLOCKS):
+            order = arriving[: as_they_arrive[i]] + arriving[as_they_arrive[i] :][::-1]
+            for b in order:
                 nc.tensor.matmul(
                     bank[:],
-                    weights[:, b, :],
+                    weights[b],
                     blocks[b][:].indirect(piece_offsets),
-                    start=(b == 0),
-                    stop=(b == K_BLOCKS - 1),
+                    start=(b == order[0]),
+                    stop=(b == order[-1]),
                 )
             staged = held.tile([P, size], F32, name=f"staged{i}")
             nc.vector.tensor_copy(staged[:], bank[:])

@@ -21,20 +21,21 @@ def tile_gather_matmul_kernel(tc, table, w, offs, out):
         tc.tile_pool(name="held", bufs=1) as held,
         tc.psum_pool(name="psum", bufs=1) as psum,
     ):
-        offsets = held.tile([P, N // 16], U16, name="offsets")
-        nc.sync.dma_start(offsets[:], offs)
 
         blocks = [held.tile([P, S], BF16, name=f"block{b}") for b in range(K_BLOCKS)]
-        nc.scalar.dma_start(blocks[0][:], table[0:P, :])
+        nc.sync.dma_start(blocks[0][:], table[0:P, :])
+
+        offsets = held.tile([P, N // 16], U16, name="offsets")
+        nc.sync.dma_start(offsets[:], offs)
 
         first_weights = held.tile([P, M], BF16, name="first_weights")
         nc.sync.dma_start(first_weights[:], w[0:P, :])
         later_weights = held.tile([P, K_BLOCKS - 1, M], BF16, name="later_weights")
-        nc.scalar.dma_start(later_weights[:], w[P:K, :].rearrange("(b p) m -> p b m", p=P))
+        nc.sync.dma_start(later_weights[:], w[P:K, :].rearrange("(b p) m -> p b m", p=P))
         weights = [first_weights[:]] + [later_weights[:, b - 1, :] for b in range(1, K_BLOCKS)]
 
         for b in range(1, K_BLOCKS):
-            nc.scalar.dma_start(blocks[b][:], table[b * P : (b + 1) * P, :])
+            nc.sync.dma_start(blocks[b][:], table[b * P : (b + 1) * P, :])
 
         arriving = list(range(K_BLOCKS))
         as_they_arrive = (K_BLOCKS, 1, 0)

@@ -54,6 +54,6 @@ def tile_gather_matmul_kernel(tc, table, w, offs, out):
                 )
             staged = held.tile([P, size], F32, name=f"staged{i}")
             nc.vector.tensor_copy(staged[:], bank[:])
-            queue = nc.sync if i % 2 == 0 else nc.scalar
+            queue = nc.sync if i == len(PIECES) - 1 else nc.scalar
             queue.dma_start(out[:, first : first + size], staged[:])
             first += size

@@ -11,6 +11,7 @@ K_BLOCKS = K // P
 BANK = 512
 PIECES = (512, 384, 128)
 assert sum(PIECES) == N and max(PIECES) <= BANK
+PARTS = (2, 2, 1)
 
 FLOPS = 2 * K * M * N
 
@@ -52,8 +53,10 @@ def tile_gather_matmul_kernel(tc, table, w, offs, out):
                     start=(b == order[0]),
                     stop=(b == order[-1]),
                 )
-            staged = held.tile([P, size], F32, name=f"staged{i}")
-            nc.vector.tensor_copy(staged[:], bank[:])
             queue = nc.sync if i == len(PIECES) - 1 else nc.scalar
-            queue.dma_start(out[:, first : first + size], staged[:])
-            first += size
+            width = size // PARTS[i]
+            for part in range(PARTS[i]):
+                staged = held.tile([P, width], F32, name=f"staged{i}_{part}")
+                nc.vector.tensor_copy(staged[:], bank[:, part * width : (part + 1) * width])
+                queue.dma_start(out[:, first : first + width], staged[:])
+                first += width

@@ -11,6 +11,7 @@ K_BLOCKS = K // P
 BANK = 512
 PIECES = (512, 384, 128)
 assert sum(PIECES) == N and max(PIECES) <= BANK
+ROW_ALIGN = 256
 PARTS = (2, 2, 1)
 
 FLOPS = 2 * K * M * N
@@ -23,15 +24,20 @@ def tile_gather_matmul_kernel(tc, table, w, offs, out):
         tc.psum_pool(name="psum", bufs=1) as psum,
     ):
 
-        blocks = [held.tile([P, S], BF16, name=f"block{b}") for b in range(K_BLOCKS)]
+        blocks = [
+            held.tile([P, S], BF16, name=f"block{b}", align_bytes=ROW_ALIGN)
+            for b in range(K_BLOCKS)
+        ]
         nc.sync.dma_start(blocks[0][:], table[0:P, :])
 
-        offsets = held.tile([P, N // 16], U16, name="offsets")
+        offsets = held.tile([P, N // 16], U16, name="offsets", align_bytes=ROW_ALIGN)
         nc.sync.dma_start(offsets[:], offs)
 
-        first_weights = held.tile([P, M], BF16, name="first_weights")
+        first_weights = held.tile([P, M], BF16, name="first_weights", align_bytes=ROW_ALIGN)
         nc.sync.dma_start(first_weights[:], w[0:P, :])
-        later_weights = held.tile([P, K_BLOCKS - 1, M], BF16, name="later_weights")
+        later_weights = held.tile(
+            [P, K_BLOCKS - 1, M], BF16, name="later_weights", align_bytes=ROW_ALIGN
+        )
         nc.sync.dma_start(later_weights[:], w[P:K, :].rearrange("(b p) m -> p b m", p=P))
         weights = [first_weights[:]] + [later_weights[:, b - 1, :] for b in range(1, K_BLOCKS)]
 
@@ -56,7 +62,9 @@ def tile_gather_matmul_kernel(tc, table, w, offs, out):
             queue = nc.sync if i == len(PIECES) - 1 else nc.scalar
             width = size // PARTS[i]
             for part in range(PARTS[i]):
-                staged = held.tile([P, width], F32, name=f"staged{i}_{part}")
+                staged = held.tile(
+                    [P, width], F32, name=f"staged{i}_{part}", align_bytes=ROW_ALIGN
+                )
                 nc.vector.tensor_copy(staged[:], bank[:, part * width : (part + 1) * width])
                 queue.dma_start(out[:, first : first + width], staged[:])
                 first += width

@@ -12,7 +12,7 @@ BANK = 512
 PIECES = (512, 384, 128)
 assert sum(PIECES) == N and max(PIECES) <= BANK
 ROW_ALIGN = 256
-PARTS = (2, 2, 1)
+PARTS = (1, 2, 2)
 
 FLOPS = 2 * K * M * N
 
@@ -59,12 +59,12 @@ def tile_gather_matmul_kernel(tc, table, w, offs, out):
                     start=(b == order[0]),
                     stop=(b == order[-1]),
                 )
-            queue = nc.sync if i == len(PIECES) - 1 else nc.scalar
             width = size // PARTS[i]
             for part in range(PARTS[i]):
                 staged = held.tile(
                     [P, width], F32, name=f"staged{i}_{part}", align_bytes=ROW_ALIGN
                 )
                 nc.vector.tensor_copy(staged[:], bank[:, part * width : (part + 1) * width])
+                queue = nc.sync if first + width == N else nc.scalar
                 queue.dma_start(out[:, first : first + width], staged[:])
                 first += width

@@ -12,7 +12,7 @@ BANK = 512
 PIECES = (512, 384, 128)
 assert sum(PIECES) == N and max(PIECES) <= BANK
 ROW_ALIGN = 256
-PARTS = (1, 2, 2)
+PARTS = (2, 3, 2)
 
 FLOPS = 2 * K * M * N
 

@@ -65,6 +65,5 @@ def tile_gather_matmul_kernel(tc, table, w, offs, out):
                     [P, width], F32, name=f"staged{i}_{part}", align_bytes=ROW_ALIGN
                 )
                 nc.vector.tensor_copy(staged[:], bank[:, part * width : (part + 1) * width])
-                queue = nc.sync if first + width == N else nc.scalar
-                queue.dma_start(out[:, first : first + width], staged[:])
+                nc.sync.dma_start(out[:, first : first + width], staged[:])
                 first += width

@@ -59,11 +59,14 @@ def tile_gather_matmul_kernel(tc, table, w, offs, out):
                     start=(b == order[0]),
                     stop=(b == order[-1]),
                 )
+            last = i == len(PIECES) - 1
+            copy = nc.scalar.copy if last else nc.vector.tensor_copy
+            queue = nc.scalar if last else nc.sync
             width = size // PARTS[i]
             for part in range(PARTS[i]):
                 staged = held.tile(
                     [P, width], F32, name=f"staged{i}_{part}", align_bytes=ROW_ALIGN
                 )
-                nc.vector.tensor_copy(staged[:], bank[:, part * width : (part + 1) * width])
-                nc.sync.dma_start(out[:, first : first + width], staged[:])
+                copy(staged[:], bank[:, part * width : (part + 1) * width])
+                queue.dma_start(out[:, first : first + width], staged[:])
                 first += width

import concourse.mybir as mybir

BF16, F32, U16 = mybir.dt.bfloat16, mybir.dt.float32, mybir.dt.uint16

P = 128
S = 1024
K = 512
M = 128
N = 1024
K_BLOCKS = K // P
BANK = 512
PIECES = (512, 384, 128)
assert sum(PIECES) == N and max(PIECES) <= BANK
ROW_ALIGN = 256
PARTS = (2, 3, 2)

FLOPS = 2 * K * M * N


def tile_gather_matmul_kernel(tc, table, w, offs, out):
    nc = tc.nc
    with (
        tc.tile_pool(name="held", bufs=1) as held,
        tc.psum_pool(name="psum", bufs=1) as psum,
    ):

        blocks = [
            held.tile([P, S], BF16, name=f"block{b}", align_bytes=ROW_ALIGN)
            for b in range(K_BLOCKS)
        ]
        nc.sync.dma_start(blocks[0][:], table[0:P, :])

        offsets = held.tile([P, N // 16], U16, name="offsets", align_bytes=ROW_ALIGN)
        nc.sync.dma_start(offsets[:], offs)

        first_weights = held.tile([P, M], BF16, name="first_weights", align_bytes=ROW_ALIGN)
        nc.sync.dma_start(first_weights[:], w[0:P, :])
        later_weights = held.tile(
            [P, K_BLOCKS - 1, M], BF16, name="later_weights", align_bytes=ROW_ALIGN
        )
        nc.sync.dma_start(later_weights[:], w[P:K, :].rearrange("(b p) m -> p b m", p=P))
        weights = [first_weights[:]] + [later_weights[:, b - 1, :] for b in range(1, K_BLOCKS)]

        for b in range(1, K_BLOCKS):
            nc.sync.dma_start(blocks[b][:], table[b * P : (b + 1) * P, :])

        arriving = list(range(K_BLOCKS))
        as_they_arrive = (K_BLOCKS, 1, 0)
        first = 0
        for i, size in enumerate(PIECES):
            piece_offsets = offsets[:, first // 16 : (first + size) // 16]
            bank = psum.tile([P, size], F32, name=f"bank{i}")
            order = arriving[: as_they_arrive[i]] + arriving[as_they_arrive[i] :][::-1]
            for b in order:
                nc.tensor.matmul(
                    bank[:],
                    weights[b],
                    blocks[b][:].indirect(piece_offsets),
                    start=(b == order[0]),
                    stop=(b == order[-1]),
                )
            last = i == len(PIECES) - 1
            copy = nc.scalar.copy if last else nc.vector.tensor_copy
            queue = nc.scalar if last else nc.sync
            width = size // PARTS[i]
            for part in range(PARTS[i]):
                staged = held.tile(
                    [P, width], F32, name=f"staged{i}_{part}", align_bytes=ROW_ALIGN
                )
                copy(staged[:], bank[:, part * width : (part + 1) * width])
                queue.dma_start(out[:, first : first + width], staged[:])
                first += width
